import numpy as np
import ml_dtypes


def mxq(x, axis, fmt="e4m3"):
    dtype, down = {"e4m3": (ml_dtypes.float8_e4m3fn, 7), "e5m2": (ml_dtypes.float8_e5m2, 14)}[fmt]
    v = np.moveaxis(np.asarray(x, np.float32).astype(ml_dtypes.bfloat16).astype(np.float64), axis, -1)
    blocks = v.reshape(v.shape[:-1] + (-1, 32))
    amax = np.abs(blocks).max(-1, keepdims=True)
    byte = np.maximum(np.where(amax > 0, np.frexp(amax)[1] - 1 + 127, 0) - down, 1)
    scale = np.exp2(byte - 127.0)
    codes = (blocks / scale).astype(np.float32).astype(dtype).astype(np.float64)
    return np.moveaxis((codes * scale).reshape(v.shape), -1, axis)


WIDE = False


def mx_kscale(k):
    if not WIDE:
        return np.ones(k)
    levels = np.array([10, -10, 5, -5, 0])
    if k % 512:
        return np.exp2(np.random.permutation(np.resize(levels, k // 32))).repeat(32)
    a = np.empty((k // 512, 16))
    for p in range(k // 512):
        a[p, :8] = np.random.permutation(np.resize(levels, 8))
        for g in range(8):
            far = levels[np.abs(levels - a[p, g]) >= 10]
            a[p, g + 8] = far[np.random.randint(len(far))]
    return np.exp2(a.ravel()).repeat(32)


def f64(x):
    return np.asarray(x).astype(np.float64)


def striped(idx):
    return np.tile(np.asarray(idx).reshape(-1, 16).T, (8, 1)).astype(np.uint16)


def unstriped(offs):
    return offs[:16].T.reshape(-1).astype(np.int64)


E2M1 = np.array([0.0, 0.5, 1.0, 1.5, 2.0, 3.0, 4.0, 6.0, -0.0, -0.5, -1.0, -1.5, -2.0, -3.0, -4.0, -6.0])


def pack_weight(w, fmt):
    k, n = w.shape
    w = f64(np.asarray(w, np.float32).astype(ml_dtypes.bfloat16)).reshape(k // 32, 32, n)
    amax = np.abs(w).max(1)
    if fmt == "e4m3":
        byte = np.frexp(amax)[1] - 1 + 127 - 7
    else:
        mant, ex = np.frexp(amax / 6.0)
        byte = np.where(mant > 0.5, ex, ex - 1) + 127
    byte = np.clip(np.where(amax > 0, byte, 1), 1, 254)
    scaled = (w * np.exp2(127.0 - byte)[:, None, :]).reshape(k, n).astype(np.float32)
    by_word = np.ascontiguousarray(scaled.reshape(k // 512, 128, 4, n).transpose(0, 1, 3, 2))
    if fmt == "e4m3":
        words = by_word.astype(ml_dtypes.float8_e4m3fn).view(np.uint8)
    else:
        c = by_word.astype(ml_dtypes.float4_e2m1fn).view(np.uint8) & 0xF
        words = (c[..., 0::2] | (c[..., 1::2] << 4)).reshape(k // 512, 128, 2 * n)
    return np.ascontiguousarray(words), np.ascontiguousarray(byte.astype(np.uint8).reshape(k // 512, 16, n))


def unpack_weight(words, scales, fmt):
    g, _, n = scales.shape
    words = np.ascontiguousarray(words).reshape(g, 128, n, -1)
    if fmt == "e4m3":
        vals = words.view(ml_dtypes.float8_e4m3fn).astype(np.float64)
    else:
        nib = np.empty((g, 128, n, 4), np.uint8)
        nib[..., 0::2] = words & 0xF
        nib[..., 1::2] = words >> 4
        vals = E2M1[nib]
    vals = vals * np.repeat(np.exp2(scales.astype(np.float64) - 127.0), 8, axis=1)[..., None]
    return vals.transpose(0, 1, 3, 2).reshape(g * 512, n)


D, T, I, Q, E, G = 512, 2048, 512, 128, 512, 64


def setup_inputs():
    n = np.random.standard_normal
    idx = np.random.permutation(T)[:I]
    fd = mx_kscale(D)
    fi = mx_kscale(I)
    ti = np.ones(T)
    ti[idx] = fi
    keysp = pack_weight(n((D, T)) / fd[:, None], "e4m3")
    return {
        "query": (n((D, Q)) * 0.8 / np.sqrt(D) * fd[:, None]).astype(np.float32),
        "keys_words": keysp[0],
        "keys_scales": keysp[1],
        "lam": (np.random.uniform(0.3, 0.9, (1, Q))).astype(np.float32),
        "shy": (np.random.uniform(20.0, 60.0, (Q, 1))).astype(np.float32),
        "os": (np.random.uniform(4.0, 16.0, (1, I)) * fi).astype(np.float32),
        "vals": (n((E, T)) / ti).astype(np.float32),
        "target": (n((Q, E))).astype(np.float32),
        "offs": striped(idx),
    }


def reference(query, keys_words, keys_scales, lam, shy, os, vals, target, offs):
    idx = unstriped(offs)
    keysu = unpack_weight(keys_words, keys_scales, "e4m3")
    keysidxg = keysu[:, idx]
    queryq = mxq(f64(query), 0, "e4m3")
    a0 = keysidxg.T @ queryq
    a1p = np.pad(a0, ((0, 0), (1, 0)))[:, :Q]
    s0 = a0 + np.tanh(a1p) * f64(lam)
    s = s0.T
    p = np.exp(s - np.max(s, axis=1, keepdims=True))
    r = p / np.sum(p, axis=1, keepdims=True)
    pg = r.reshape(Q, G, I // G).sum(axis=2)
    k0 = np.exp(pg * f64(shy) * (-1.0))
    kr = np.repeat(k0, I // G, axis=1)
    u0 = r * kr
    w = u0 / np.sum(u0, axis=1, keepdims=True)
    wo1 = w * f64(os)
    wt1 = wo1.T
    vt1 = f64(vals)[:, idx].T
    wt1q = mxq(wt1, 0, "e4m3")
    vt1q = mxq(vt1, 0, "e4m3")
    o = wt1q.T @ vt1q
    rs = f64(target) - o
    k2 = np.sqrt(np.mean(np.square(rs), axis=1, keepdims=True) + 0.5)
    y = rs / k2
    return y

@@ -1,0 +1,317 @@
+from contextlib import ExitStack
+
+import concourse.mybir as mybir
+
+D, T, I, Q, E, G = 512, 2048, 512, 128, 512, 64
+FLOPS = 2 * D * I * Q + 2 * I * Q * E
+
+F32 = mybir.dt.float32
+BF16 = mybir.dt.bfloat16
+I32 = mybir.dt.int32
+U32 = mybir.dt.uint32
+U16 = mybir.dt.uint16
+U8 = mybir.dt.uint8
+FP8X4 = mybir.dt.float8_e4m3fn_x4
+ALU = mybir.AluOpType
+ACT = mybir.ActivationFunctionType
+AX = mybir.AxisListType
+
+P = 128
+PACK = 4
+RUN = I // G
+HALF = I // 2
+PER_COL = 16
+BLOCKS = E // P
+LAST_ON_SCALAR = 256
+
+
+def tile_attend_afterprevious_crowdshy_remainder_kernel(
+    tc, query, keys_words, keys_scales, lam, shy, slot_factor, vals, target, offs, out
+):
+    nc = tc.nc
+    with ExitStack() as ctx:
+        keep = ctx.enter_context(tc.tile_pool(name="keep", bufs=1))
+        psum = ctx.enter_context(tc.psum_pool(name="psum", bufs=1))
+
+        offsets = keep.tile([P, I // PER_COL], U16, name="offsets")
+        nc.sync.dma_start(offsets[:], offs)
+
+        def listed(window, first, last):
+            return window[:].indirect(offsets[:, first // PER_COL : last // PER_COL])
+
+        key_scales = keep.tile([P, T], U8, name="key_scales", align_bytes=64)
+        nc.vector.memset(key_scales[:].bitcast(I32), 0)
+        q_raw = keep.tile([P, PACK, Q], F32, name="q_raw", align_bytes=64)
+        nc.sync.dma_start(q_raw[:], query.rearrange("(p t) q -> p t q", t=PACK))
+        for quad in range(4):
+            queue = nc.sync if quad < 2 else nc.scalar
+            queue.dma_start(
+                key_scales[32 * quad : 32 * quad + 4, :].bitcast(I32),
+                keys_scales[0, 4 * quad : 4 * quad + 4, :].bitcast(I32),
+            )
+
+        ident = keep.tile([P, P], F32, name="ident", align_bytes=64)
+        with tc.tile_pool(name="first", bufs=1) as first_pool:
+            zeros = first_pool.tile([P, P], F32, name="zeros", offset=4 * T)
+            nc.gpsimd.memset(zeros[:], 0.0)
+            nc.gpsimd.affine_select(
+                out=ident[:], in_=zeros[:], pattern=[[-1, P]], compare_op=ALU.not_equal, fill=1.0,
+                base=0, channel_multiplier=1,
+            )
+
+        last = ctx.enter_context(tc.tile_pool(name="last", bufs=1))
+        work = ctx.enter_context(tc.tile_pool(name="work", bufs=1))
+
+        def sbuf(shape, dtype, name, tag=None):
+            return work.tile(shape, dtype, name=name, tag=tag or name, align_bytes=64)
+
+        key_words = sbuf([P, T], U32, "key_words")
+        nc.sync.dma_start(
+            key_words[:].bitcast(I32),
+            keys_words[0].rearrange("p n t -> p (n t)").bitcast(I32),
+        )
+        lam_col = sbuf([Q, 1], F32, "lam_col")
+        shy_col = sbuf([Q, 1], F32, "shy_col")
+        os_col = sbuf([P, PACK], F32, "os_col")
+        with nc.allow_non_contiguous_dma(reason="one value a partition"):
+            nc.sync.dma_start(lam_col[:], lam.rearrange("o q -> q o"))
+        val_pool = []
+        for b in range(BLOCKS):
+            if b < BLOCKS - 1:
+                block = sbuf([P, T], F32, f"val_pool{b}")
+            else:
+                block = last.tile([P, T], F32, name=f"val_pool{b}", align_bytes=64, offset=0)
+            nc.sync.dma_start(block[:], vals[P * b : P * (b + 1), :])
+            val_pool.append(block)
+            if b == 0:
+                with nc.allow_non_contiguous_dma(reason="one value a partition"):
+                    nc.sync.dma_start(shy_col[:], shy)
+                nc.sync.dma_start(os_col[:], slot_factor.rearrange("o (p t) -> p (o t)", t=PACK))
+        target_sb = sbuf([Q, E], F32, "target_sb")
+        nc.sync.dma_start(target_sb[:], target)
+
+        kg_scales = sbuf([P, I], U8, "kg_scales")
+        nc.vector.tensor_copy(kg_scales[:], listed(key_scales, 0, I))
+
+        def quantise(grouped, codes, scales):
+            nc.vector.quantize_mx(
+                out=codes.bitcast(FP8X4), scales=scales, in_=grouped.rearrange("p c t -> p (c t)")
+            )
+
+        q_grouped = sbuf([P, Q, PACK], BF16, "q_grouped")
+        nc.scalar.copy(
+            q_grouped[:].rearrange("p (c i) t -> p c t i", i=4),
+            q_raw[:].rearrange("p t (c i) -> p c t i", i=4),
+        )
+        q_codes = sbuf([P, Q], U32, "q_codes")
+        q_scales = sbuf([P, Q], U8, "q_scales")
+        quantise(q_grouped[:], q_codes[:], q_scales[:])
+
+        lam_tanh = sbuf([P, I // P, Q], F32, "lam_tanh")
+        nc.vector.memset(lam_tanh[:, :, 0:1], 0.0)
+
+        lam_rows = psum.tile([P, Q], F32, name="lam_rows", tag="bank_w")
+        nc.tensor.transpose(lam_rows[:], lam_col[:].to_broadcast([Q, P]), ident[:])
+
+        a0_banks = []
+        for h in range(2):
+            kg_words = sbuf([P, HALF], U32, f"kg_words{h}")
+            nc.vector.tensor_copy(kg_words[:], listed(key_words, HALF * h, HALF * (h + 1)))
+            a0 = psum.tile([P, 2, Q], F32, name=f"a0_{h}", tag=f"bank_a{h}")
+            for j in range(2):
+                slots = slice(HALF * h + P * j, HALF * h + P * (j + 1))
+                nc.tensor.matmul_mx(
+                    out=a0[:, j, :],
+                    lhsT=kg_words[:, P * j : P * (j + 1)].bitcast(FP8X4),
+                    lhsT_scale=kg_scales[:, slots],
+                    rhs=q_codes[:].bitcast(FP8X4),
+                    rhs_scale=q_scales[:],
+                    start=True,
+                    stop=True,
+                )
+            a0_banks.append(a0)
+
+
+        a0_sb = sbuf([P, I // P, Q], F32, "a0_sb")
+        s_banks = []
+        for h in range(2):
+            tiles = slice(2 * h, 2 * h + 2)
+            tanh_sb = sbuf([P, 2, Q], F32, f"tanh_sb{h}")
+            nc.scalar.activation(tanh_sb[:], a0_banks[h][:], ACT.Tanh)
+            copy = nc.scalar.copy if h == 0 else nc.vector.tensor_copy
+            copy(a0_sb[:, tiles, :], a0_banks[h][:])
+            nc.vector.tensor_tensor(
+                lam_tanh[:, tiles, 1:Q],
+                tanh_sb[:, :, 0 : Q - 1],
+                lam_rows[:, 1:Q].unsqueeze(1).to_broadcast([P, 2, Q - 1]),
+                ALU.mult,
+            )
+            s_bank = psum.tile([Q, 2, P], F32, name=f"s_{h}", tag=f"bank_s{h}")
+            for n, src in enumerate((a0_sb, lam_tanh)):
+                for j in range(2):
+                    nc.tensor.matmul(
+                        s_bank[:, j, :],
+                        src[:, 2 * h + j, :],
+                        ident[:],
+                        is_transpose=True,
+                        start=(n == 0 and j == 0),
+                        stop=(n == 1 and j == 1),
+                    )
+            s_banks.append(s_bank)
+
+        neg_s = sbuf([Q, I], F32, "neg_s")
+        neg_max = [sbuf([Q, 1], F32, f"neg_max{h}") for h in range(2)]
+        for h in range(2):
+            nc.vector.tensor_scalar(
+                neg_s[:, HALF * h : HALF * (h + 1)],
+                s_banks[h][:].rearrange("q j p -> q (j p)"),
+                -1.0,
+                None if h == 0 else neg_max[0][:],
+                ALU.mult,
+                ALU.min,
+                accum_out=neg_max[h][:],
+            )
+
+        os_rows = psum.tile([P, PACK, P], F32, name="os_rows", tag="bank_s0")
+        for t in range(PACK):
+            nc.tensor.transpose(os_rows[:, t, :], os_col[:, t : t + 1].to_broadcast([P, P]), ident[:])
+        inv_shy = sbuf([Q, 1], F32, "inv_shy", tag="tanh_sb1")
+        nc.vector.reciprocal(inv_shy[:], shy_col[:])
+        neg_inv_shy = sbuf([Q, 1], F32, "neg_inv_shy")
+        nc.vector.tensor_scalar(neg_inv_shy[:], inv_shy[:], -1.0, None, ALU.mult)
+
+        def gather_on_scalar(gathered, b, first, last):
+            nc.scalar.activation(gathered[:, first:last], listed(val_pool[b], first, last), ACT.Copy)
+
+        def turn(src, bank_tag, name):
+            words = src[:].bitcast(F32)
+            turned = psum.tile([P, 2, P], F32, name=f"{name}_turned", tag=bank_tag)
+            for u in range(2):
+                nc.tensor.transpose(turned[:, u, :], words[:, u : I // 2 : 2], ident[:])
+            return turned
+
+        def weave(copy, grouped, turned):
+            copy(grouped.bitcast(F32), turned[:].rearrange("p u c -> p c u"))
+
+        gathered0 = sbuf([P, I], BF16, "gathered0", tag="tanh_sb0")
+        gather_on_scalar(gathered0, 0, 0, I)
+
+        p_sb = sbuf([Q, I], F32, "p_sb", tag="val_pool0")
+        p_sum = [sbuf([Q, 1], F32, f"p_sum{h}") for h in range(2)]
+        run_sum = sbuf([Q, G], F32, "run_sum")
+        for h in range(2):
+            cols = slice(HALF * h, HALF * (h + 1))
+            nc.scalar.activation(
+                p_sb[:, cols], neg_s[:, cols], ACT.Exp, bias=neg_max[1][:], scale=-1.0, accum_out=p_sum[h][:]
+            )
+        gathered1 = sbuf([P, I], BF16, "gathered1", tag="neg_s")
+        gather_on_scalar(gathered1, 1, 0, I)
+        pair = 2 * P
+        v01_grouped = sbuf([P, pair, PACK], BF16, "v01_grouped")
+        weave(nc.vector.tensor_copy, v01_grouped[:, 0:P, :], turn(gathered0, "bank_s1", "v0"))
+        v1_turned = turn(gathered1, "bank_a0", "v1")
+
+        def sum_runs(h):
+            nc.vector.tensor_reduce(
+                run_sum[:, (G // 2) * h : (G // 2) * (h + 1)],
+                p_sb[:, HALF * h : HALF * (h + 1)].rearrange("q (g r) -> q g r", r=RUN),
+                AX.X,
+                ALU.add,
+            )
+
+        sum_runs(0)
+        total = sbuf([Q, 1], F32, "total")
+        nc.vector.tensor_scalar(total[:], p_sum[0][:], p_sum[1][:], neg_inv_shy[:], ALU.add, ALU.mult)
+        sum_runs(1)
+        damp_rate = sbuf([Q, 1], F32, "damp_rate")
+        nc.vector.reciprocal(damp_rate[:], total[:])
+        damp = sbuf([Q, G], F32, "damp", tag="val_pool1")
+        nc.scalar.activation(damp[:], run_sum[:], ACT.Exp, scale=damp_rate[:])
+        gathered2 = sbuf([P, I], BF16, "gathered2", tag="damp_rate")
+        gather_on_scalar(gathered2, 2, 0, I)
+        p_os = sbuf([Q, I], F32, "p_os")
+        nc.vector.tensor_tensor(
+            p_os[:].rearrange("q (p t) -> q p t", t=PACK),
+            p_sb[:].rearrange("q (p t) -> q p t", t=PACK),
+            os_rows[:].rearrange("q t p -> q p t"),
+            ALU.mult,
+        )
+        damped_runs = sbuf([Q, G], F32, "damped_runs")
+        damped_sum = sbuf([Q, 1], F32, "damped_sum")
+        nc.vector.scalar_tensor_tensor(
+            damped_runs[:], run_sum[:], 1.0, damp[:], ALU.mult, ALU.mult, accum_out=damped_sum[:]
+        )
+        inv_damped = sbuf([Q, 1], F32, "inv_damped")
+        nc.vector.reciprocal(inv_damped[:], damped_sum[:])
+        w_bf = sbuf([Q, I], BF16, "w_bf", tag="neg_s")
+        nc.vector.scalar_tensor_tensor(
+            w_bf[:].rearrange("q (g r) -> q g r", r=RUN),
+            p_os[:].rearrange("q (g r) -> q g r", r=RUN),
+            inv_damped[:],
+            damp[:].unsqueeze(2).to_broadcast([Q, G, RUN]),
+            ALU.mult,
+            ALU.mult,
+        )
+
+        weave(nc.vector.tensor_copy, v01_grouped[:, P:pair, :], v1_turned)
+        v01_codes = sbuf([P, pair], U32, "v01_codes")
+        v01_scales = sbuf([P, pair], U8, "v01_scales")
+        quantise(v01_grouped[:], v01_codes[:], v01_scales[:])
+        v2_grouped = sbuf([P, P, PACK], BF16, "v2_grouped")
+        weave(nc.scalar.copy, v2_grouped[:], turn(gathered2, "bank_a1", "v2"))
+        w_turned = turn(w_bf, "bank_a1", "w")
+
+        gathered3 = sbuf([P, I], BF16, "gathered3")
+        gather_on_scalar(gathered3, 3, 0, LAST_ON_SCALAR)
+        nc.vector.tensor_copy(gathered3[:, LAST_ON_SCALAR:I], listed(val_pool[3], LAST_ON_SCALAR, I))
+        v3_turned = turn(gathered3, "bank_w", "v3")
+
+        w_grouped = last.tile([P, Q, PACK], BF16, name="w_grouped", align_bytes=64, offset=0)
+        weave(nc.scalar.copy, w_grouped[:], w_turned)
+        v2_codes = last.tile([P, P], U32, name="v2_codes", align_bytes=64, offset=2 * PACK * Q)
+        v2_scales = sbuf([P, P], U8, "v2_scales")
+        quantise(v2_grouped[:], v2_codes[:], v2_scales[:])
+        w_codes = sbuf([P, Q], U32, "w_codes")
+        w_scales = sbuf([P, Q], U8, "w_scales")
+        quantise(w_grouped[:], w_codes[:], w_scales[:])
+
+        def product(bank, codes, scales):
+            nc.tensor.matmul_mx(
+                out=bank,
+                lhsT=w_codes[:].bitcast(FP8X4),
+                lhsT_scale=w_scales[:],
+                rhs=codes[:].bitcast(FP8X4),
+                rhs_scale=scales[:],
+                start=True,
+                stop=True,
+            )
+
+        early = E - P
+        o_early = psum.tile([Q, early], F32, name="o_early", tag="bank_s1")
+        product(o_early[:, 0:pair], v01_codes, v01_scales)
+        product(o_early[:, pair:early], v2_codes, v2_scales)
+
+        v3_grouped = sbuf([P, P, PACK], BF16, "v3_grouped")
+        weave(nc.vector.tensor_copy, v3_grouped[:], v3_turned)
+        v3_codes = sbuf([P, P], U32, "v3_codes")
+        v3_scales = sbuf([P, P], U8, "v3_scales")
+        quantise(v3_grouped[:], v3_codes[:], v3_scales[:])
+        o_late = psum.tile([Q, P], F32, name="o_late", tag="bank_s0")
+        product(o_late[:], v3_codes, v3_scales)
+
+        rest = sbuf([Q, E + 1], F32, "rest", tag="v3_grouped")
+        nc.gpsimd.memset(rest[:, E : E + 1], 16.0)
+        minus_half = sbuf([Q, 1], F32, "minus_half")
+        nc.gpsimd.memset(minus_half[:], -0.5)
+        nc.vector.tensor_tensor(rest[:, 0:early], target_sb[:, 0:early], o_early[:], ALU.subtract)
+        nc.vector.tensor_tensor(rest[:, early:E], target_sb[:, early:E], o_late[:], ALU.subtract)
+        squares = sbuf([Q, E + 1], F32, "squares")
+        mean_sq = sbuf([Q, 1], F32, "mean_sq")
+        nc.vector.scalar_tensor_tensor(
+            squares[:], rest[:], 1.0 / E, rest[:], ALU.mult, ALU.mult, accum_out=mean_sq[:]
+        )
+        inv_norm = sbuf([Q, 1], F32, "inv_norm")
+        nc.gpsimd.tensor_tensor(inv_norm[:], mean_sq[:], minus_half[:], ALU.pow)
+        result = sbuf([Q, E], F32, "result")
+        nc.vector.tensor_scalar(result[:], rest[:, 0:E], inv_norm[:], None, ALU.mult)
+        nc.sync.dma_start(out, result[:])

@@ -22,6 +22,7 @@ RUN = I // G
 HALF = I // 2
 PER_COL = 16
 BLOCKS = E // P
+SECOND_ON_SCALAR = 384
 LAST_ON_SCALAR = 256
 
 
@@ -81,7 +82,8 @@ def tile_attend_afterprevious_crowdshy_remainder_kernel(
                 block = sbuf([P, T], F32, f"val_pool{b}")
             else:
                 block = last.tile([P, T], F32, name=f"val_pool{b}", align_bytes=64, offset=0)
-            nc.sync.dma_start(block[:], vals[P * b : P * (b + 1), :])
+            first_row = P * ((b + 1) % BLOCKS)
+            nc.sync.dma_start(block[:], vals[first_row : first_row + P, :])
             val_pool.append(block)
             if b == 0:
                 with nc.allow_non_contiguous_dma(reason="one value a partition"):
@@ -133,21 +135,29 @@ def tile_attend_afterprevious_crowdshy_remainder_kernel(
 
 
         a0_sb = sbuf([P, I // P, Q], F32, "a0_sb")
-        s_banks = []
+        tanh_sb = [sbuf([P, 2, Q], F32, f"tanh_sb{h}") for h in range(2)]
         for h in range(2):
-            tiles = slice(2 * h, 2 * h + 2)
-            tanh_sb = sbuf([P, 2, Q], F32, f"tanh_sb{h}")
-            nc.scalar.activation(tanh_sb[:], a0_banks[h][:], ACT.Tanh)
-            copy = nc.scalar.copy if h == 0 else nc.vector.tensor_copy
-            copy(a0_sb[:, tiles, :], a0_banks[h][:])
+            nc.scalar.activation(tanh_sb[h][:], a0_banks[h][:], ACT.Tanh)
+
+        def copy_products(h):
+            nc.vector.tensor_copy(a0_sb[:, 2 * h : 2 * h + 2, :], a0_banks[h][:])
+
+        def scale_tanh(h):
             nc.vector.tensor_tensor(
-                lam_tanh[:, tiles, 1:Q],
-                tanh_sb[:, :, 0 : Q - 1],
+                lam_tanh[:, 2 * h : 2 * h + 2, 1:Q],
+                tanh_sb[h][:, :, 0 : Q - 1],
                 lam_rows[:, 1:Q].unsqueeze(1).to_broadcast([P, 2, Q - 1]),
                 ALU.mult,
             )
+
+        copy_products(0)
+        scale_tanh(0)
+        scale_tanh(1)
+        copy_products(1)
+        s_banks = []
+        for h, terms in enumerate(((a0_sb, lam_tanh), (lam_tanh, a0_sb))):
             s_bank = psum.tile([Q, 2, P], F32, name=f"s_{h}", tag=f"bank_s{h}")
-            for n, src in enumerate((a0_sb, lam_tanh)):
+            for n, src in enumerate(terms):
                 for j in range(2):
                     nc.tensor.matmul(
                         s_bank[:, j, :],
@@ -172,9 +182,6 @@ def tile_attend_afterprevious_crowdshy_remainder_kernel(
                 accum_out=neg_max[h][:],
             )
 
-        os_rows = psum.tile([P, PACK, P], F32, name="os_rows", tag="bank_s0")
-        for t in range(PACK):
-            nc.tensor.transpose(os_rows[:, t, :], os_col[:, t : t + 1].to_broadcast([P, P]), ident[:])
         inv_shy = sbuf([Q, 1], F32, "inv_shy", tag="tanh_sb1")
         nc.vector.reciprocal(inv_shy[:], shy_col[:])
         neg_inv_shy = sbuf([Q, 1], F32, "neg_inv_shy")
@@ -182,6 +189,9 @@ def tile_attend_afterprevious_crowdshy_remainder_kernel(
 
         def gather_on_scalar(gathered, b, first, last):
             nc.scalar.activation(gathered[:, first:last], listed(val_pool[b], first, last), ACT.Copy)
+
+        def gather_on_vector(gathered, b, first, last):
+            nc.vector.tensor_copy(gathered[:, first:last], listed(val_pool[b], first, last))
 
         def turn(src, bank_tag, name):
             words = src[:].bitcast(F32)
@@ -195,6 +205,12 @@ def tile_attend_afterprevious_crowdshy_remainder_kernel(
 
         gathered0 = sbuf([P, I], BF16, "gathered0", tag="tanh_sb0")
         gather_on_scalar(gathered0, 0, 0, I)
+        v0_turned = turn(gathered0, "bank_a1", "v0")
+        os_rows = psum.tile([P, PACK, P], F32, name="os_rows", tag="bank_s0")
+        for t in range(PACK):
+            nc.tensor.transpose(os_rows[:, t, :], os_col[:, t : t + 1].to_broadcast([P, P]), ident[:])
+        v0_grouped = sbuf([P, P, PACK], BF16, "v0_grouped")
+        weave(nc.vector.tensor_copy, v0_grouped[:], v0_turned)
 
         p_sb = sbuf([Q, I], F32, "p_sb", tag="val_pool0")
         p_sum = [sbuf([Q, 1], F32, f"p_sum{h}") for h in range(2)]
@@ -205,11 +221,7 @@ def tile_attend_afterprevious_crowdshy_remainder_kernel(
                 p_sb[:, cols], neg_s[:, cols], ACT.Exp, bias=neg_max[1][:], scale=-1.0, accum_out=p_sum[h][:]
             )
         gathered1 = sbuf([P, I], BF16, "gathered1", tag="neg_s")
-        gather_on_scalar(gathered1, 1, 0, I)
-        pair = 2 * P
-        v01_grouped = sbuf([P, pair, PACK], BF16, "v01_grouped")
-        weave(nc.vector.tensor_copy, v01_grouped[:, 0:P, :], turn(gathered0, "bank_s1", "v0"))
-        v1_turned = turn(gathered1, "bank_a0", "v1")
+        gather_on_scalar(gathered1, 1, 0, SECOND_ON_SCALAR)
 
         def sum_runs(h):
             nc.vector.tensor_reduce(
@@ -225,13 +237,15 @@ def tile_attend_afterprevious_crowdshy_remainder_kernel(
         sum_runs(1)
         damp_rate = sbuf([Q, 1], F32, "damp_rate")
         nc.vector.reciprocal(damp_rate[:], total[:])
-        damp = sbuf([Q, G], F32, "damp", tag="val_pool1")
-        nc.scalar.activation(damp[:], run_sum[:], ACT.Exp, scale=damp_rate[:])
+        gather_on_vector(gathered1, 1, SECOND_ON_SCALAR, I)
+        v1_turned = turn(gathered1, "bank_a0", "v1")
+        factors = sbuf([Q, I + G], F32, "factors", tag="val_pool1")
+        p_os, damp = factors[:, 0:I], factors[:, I : I + G]
+        nc.scalar.activation(damp, run_sum[:], ACT.Exp, scale=damp_rate[:])
         gathered2 = sbuf([P, I], BF16, "gathered2", tag="damp_rate")
         gather_on_scalar(gathered2, 2, 0, I)
-        p_os = sbuf([Q, I], F32, "p_os")
         nc.vector.tensor_tensor(
-            p_os[:].rearrange("q (p t) -> q p t", t=PACK),
+            p_os.rearrange("q (p t) -> q p t", t=PACK),
             p_sb[:].rearrange("q (p t) -> q p t", t=PACK),
             os_rows[:].rearrange("q t p -> q p t"),
             ALU.mult,
@@ -239,59 +253,61 @@ def tile_attend_afterprevious_crowdshy_remainder_kernel(
         damped_runs = sbuf([Q, G], F32, "damped_runs")
         damped_sum = sbuf([Q, 1], F32, "damped_sum")
         nc.vector.scalar_tensor_tensor(
-            damped_runs[:], run_sum[:], 1.0, damp[:], ALU.mult, ALU.mult, accum_out=damped_sum[:]
+            damped_runs[:], run_sum[:], 1.0, damp, ALU.mult, ALU.mult, accum_out=damped_sum[:]
         )
+        v0_codes = sbuf([P, P], U32, "v0_codes", tag="damped_runs")
+        v0_scales = sbuf([P, P], U8, "v0_scales")
+        quantise(v0_grouped[:], v0_codes[:], v0_scales[:])
         inv_damped = sbuf([Q, 1], F32, "inv_damped")
         nc.vector.reciprocal(inv_damped[:], damped_sum[:])
-        w_bf = sbuf([Q, I], BF16, "w_bf", tag="neg_s")
+        w_bf = sbuf([Q, I], BF16, "w_bf")
         nc.vector.scalar_tensor_tensor(
             w_bf[:].rearrange("q (g r) -> q g r", r=RUN),
-            p_os[:].rearrange("q (g r) -> q g r", r=RUN),
+            p_os.rearrange("q (g r) -> q g r", r=RUN),
             inv_damped[:],
-            damp[:].unsqueeze(2).to_broadcast([Q, G, RUN]),
+            damp.unsqueeze(2).to_broadcast([Q, G, RUN]),
             ALU.mult,
             ALU.mult,
         )
 
-        weave(nc.vector.tensor_copy, v01_grouped[:, P:pair, :], v1_turned)
-        v01_codes = sbuf([P, pair], U32, "v01_codes")
-        v01_scales = sbuf([P, pair], U8, "v01_scales")
-        quantise(v01_grouped[:], v01_codes[:], v01_scales[:])
-        v2_grouped = sbuf([P, P, PACK], BF16, "v2_grouped")
-        weave(nc.scalar.copy, v2_grouped[:], turn(gathered2, "bank_a1", "v2"))
-        w_turned = turn(w_bf, "bank_a1", "w")
+        w_turned = turn(w_bf, "bank_w", "w")
+        v2_turned = turn(gathered2, "bank_a1", "v2")
 
-        gathered3 = sbuf([P, I], BF16, "gathered3")
+        gathered3 = sbuf([P, I], BF16, "gathered3", tag="inv_damped")
         gather_on_scalar(gathered3, 3, 0, LAST_ON_SCALAR)
-        nc.vector.tensor_copy(gathered3[:, LAST_ON_SCALAR:I], listed(val_pool[3], LAST_ON_SCALAR, I))
-        v3_turned = turn(gathered3, "bank_w", "v3")
+        gather_on_vector(gathered3, 3, LAST_ON_SCALAR, I)
+        v3_turned = turn(gathered3, "bank_v3", "v3")
 
-        w_grouped = last.tile([P, Q, PACK], BF16, name="w_grouped", align_bytes=64, offset=0)
-        weave(nc.scalar.copy, w_grouped[:], w_turned)
-        v2_codes = last.tile([P, P], U32, name="v2_codes", align_bytes=64, offset=2 * PACK * Q)
+        v1w_grouped = last.tile([P, P + Q, PACK], BF16, name="v1w_grouped", align_bytes=64, offset=4 * E)
+        v2_grouped = last.tile([P, P, PACK], BF16, name="v2_grouped", align_bytes=64, offset=0)
+        weave(nc.scalar.copy, v1w_grouped[:, 0:P, :], v1_turned)
+        weave(nc.vector.tensor_copy, v1w_grouped[:, P : P + Q, :], w_turned)
+        weave(nc.scalar.copy, v2_grouped[:], v2_turned)
+        v1w_codes = sbuf([P, P + Q], U32, "v1w_codes")
+        v1w_scales = sbuf([P, P + Q], U8, "v1w_scales")
+        quantise(v1w_grouped[:], v1w_codes[:], v1w_scales[:])
+        v2_codes = sbuf([P, P], U32, "v2_codes")
         v2_scales = sbuf([P, P], U8, "v2_scales")
         quantise(v2_grouped[:], v2_codes[:], v2_scales[:])
-        w_codes = sbuf([P, Q], U32, "w_codes")
-        w_scales = sbuf([P, Q], U8, "w_scales")
-        quantise(w_grouped[:], w_codes[:], w_scales[:])
 
         def product(bank, codes, scales):
             nc.tensor.matmul_mx(
                 out=bank,
-                lhsT=w_codes[:].bitcast(FP8X4),
-                lhsT_scale=w_scales[:],
-                rhs=codes[:].bitcast(FP8X4),
-                rhs_scale=scales[:],
+                lhsT=v1w_codes[:, P : P + Q].bitcast(FP8X4),
+                lhsT_scale=v1w_scales[:, P : P + Q],
+                rhs=codes[:, 0:P].bitcast(FP8X4),
+                rhs_scale=scales[:, 0:P],
                 start=True,
                 stop=True,
             )
 
-        early = E - P
-        o_early = psum.tile([Q, early], F32, name="o_early", tag="bank_s1")
-        product(o_early[:, 0:pair], v01_codes, v01_scales)
-        product(o_early[:, pair:early], v2_codes, v2_scales)
+        o_early = psum.tile([Q, E - P], F32, name="o_early", tag="bank_s1")
+        for b, (codes, scales) in enumerate(
+            ((v0_codes, v0_scales), (v1w_codes, v1w_scales), (v2_codes, v2_scales))
+        ):
+            product(o_early[:, P * b : P * (b + 1)], codes, scales)
 
-        v3_grouped = sbuf([P, P, PACK], BF16, "v3_grouped")
+        v3_grouped = last.tile([P, P, PACK], BF16, name="v3_grouped", align_bytes=64, offset=0)
         weave(nc.vector.tensor_copy, v3_grouped[:], v3_turned)
         v3_codes = sbuf([P, P], U32, "v3_codes")
         v3_scales = sbuf([P, P], U8, "v3_scales")
@@ -299,19 +315,28 @@ def tile_attend_afterprevious_crowdshy_remainder_kernel(
         o_late = psum.tile([Q, P], F32, name="o_late", tag="bank_s0")
         product(o_late[:], v3_codes, v3_scales)
 
-        rest = sbuf([Q, E + 1], F32, "rest", tag="v3_grouped")
-        nc.gpsimd.memset(rest[:, E : E + 1], 16.0)
-        minus_half = sbuf([Q, 1], F32, "minus_half")
-        nc.gpsimd.memset(minus_half[:], -0.5)
-        nc.vector.tensor_tensor(rest[:, 0:early], target_sb[:, 0:early], o_early[:], ALU.subtract)
-        nc.vector.tensor_tensor(rest[:, early:E], target_sb[:, early:E], o_late[:], ALU.subtract)
-        squares = sbuf([Q, E + 1], F32, "squares")
-        mean_sq = sbuf([Q, 1], F32, "mean_sq")
-        nc.vector.scalar_tensor_tensor(
-            squares[:], rest[:], 1.0 / E, rest[:], ALU.mult, ALU.mult, accum_out=mean_sq[:]
-        )
+        rest = last.tile([Q, E], F32, name="rest", align_bytes=64, offset=0)
+        squares = sbuf([Q, E], F32, "squares")
+
+        def remainder(cols, bank):
+            nc.vector.tensor_tensor(rest[:, cols], target_sb[:, cols], bank[:], ALU.subtract)
+
+        def mean_square_part(cols, name):
+            part = sbuf([Q, 1], F32, name)
+            nc.vector.scalar_tensor_tensor(
+                squares[:, cols], rest[:, cols], 1.0 / E, rest[:, cols], ALU.mult, ALU.mult, accum_out=part[:]
+            )
+            return part
+
+        early_cols, late_cols = slice(P, E), slice(0, P)
+        remainder(early_cols, o_early)
+        mean_early = mean_square_part(early_cols, "mean_early")
+        remainder(late_cols, o_late)
+        base = sbuf([Q, 1], F32, "base")
+        nc.vector.tensor_scalar(base[:], mean_early[:], 0.5, None, ALU.add)
+        mean_late = mean_square_part(late_cols, "mean_late")
         inv_norm = sbuf([Q, 1], F32, "inv_norm")
-        nc.gpsimd.tensor_tensor(inv_norm[:], mean_sq[:], minus_half[:], ALU.pow)
+        nc.scalar.activation(inv_norm[:], mean_late[:], ACT.Abs_reciprocal_sqrt, bias=base[:])
         result = sbuf([Q, E], F32, "result")
-        nc.vector.tensor_scalar(result[:], rest[:, 0:E], inv_norm[:], None, ALU.mult)
+        nc.vector.tensor_scalar(result[:], rest[:], inv_norm[:], None, ALU.mult)
         nc.sync.dma_start(out, result[:])

from contextlib import ExitStack

import concourse.mybir as mybir

D, T, I, Q, E, G = 512, 2048, 512, 128, 512, 64
FLOPS = 2 * D * I * Q + 2 * I * Q * E

F32 = mybir.dt.float32
BF16 = mybir.dt.bfloat16
I32 = mybir.dt.int32
U32 = mybir.dt.uint32
U16 = mybir.dt.uint16
U8 = mybir.dt.uint8
FP8X4 = mybir.dt.float8_e4m3fn_x4
ALU = mybir.AluOpType
ACT = mybir.ActivationFunctionType
AX = mybir.AxisListType

P = 128
PACK = 4
RUN = I // G
HALF = I // 2
PER_COL = 16
BLOCKS = E // P
SECOND_ON_SCALAR = 384
LAST_ON_SCALAR = 256


def tile_attend_afterprevious_crowdshy_remainder_kernel(
    tc, query, keys_words, keys_scales, lam, shy, slot_factor, vals, target, offs, out
):
    nc = tc.nc
    with ExitStack() as ctx:
        keep = ctx.enter_context(tc.tile_pool(name="keep", bufs=1))
        psum = ctx.enter_context(tc.psum_pool(name="psum", bufs=1))

        offsets = keep.tile([P, I // PER_COL], U16, name="offsets")
        nc.sync.dma_start(offsets[:], offs)

        def listed(window, first, last):
            return window[:].indirect(offsets[:, first // PER_COL : last // PER_COL])

        key_scales = keep.tile([P, T], U8, name="key_scales", align_bytes=64)
        nc.vector.memset(key_scales[:].bitcast(I32), 0)
        q_raw = keep.tile([P, PACK, Q], F32, name="q_raw", align_bytes=64)
        nc.sync.dma_start(q_raw[:], query.rearrange("(p t) q -> p t q", t=PACK))
        for quad in range(4):
            queue = nc.sync if quad < 2 else nc.scalar
            queue.dma_start(
                key_scales[32 * quad : 32 * quad + 4, :].bitcast(I32),
                keys_scales[0, 4 * quad : 4 * quad + 4, :].bitcast(I32),
            )

        ident = keep.tile([P, P], F32, name="ident", align_bytes=64)
        with tc.tile_pool(name="first", bufs=1) as first_pool:
            zeros = first_pool.tile([P, P], F32, name="zeros", offset=4 * T)
            nc.gpsimd.memset(zeros[:], 0.0)
            nc.gpsimd.affine_select(
                out=ident[:], in_=zeros[:], pattern=[[-1, P]], compare_op=ALU.not_equal, fill=1.0,
                base=0, channel_multiplier=1,
            )

        last = ctx.enter_context(tc.tile_pool(name="last", bufs=1))
        work = ctx.enter_context(tc.tile_pool(name="work", bufs=1))

        def sbuf(shape, dtype, name, tag=None):
            return work.tile(shape, dtype, name=name, tag=tag or name, align_bytes=64)

        key_words = sbuf([P, T], U32, "key_words")
        nc.sync.dma_start(
            key_words[:].bitcast(I32),
            keys_words[0].rearrange("p n t -> p (n t)").bitcast(I32),
        )
        lam_col = sbuf([Q, 1], F32, "lam_col")
        shy_col = sbuf([Q, 1], F32, "shy_col")
        os_col = sbuf([P, PACK], F32, "os_col")
        with nc.allow_non_contiguous_dma(reason="one value a partition"):
            nc.sync.dma_start(lam_col[:], lam.rearrange("o q -> q o"))
        val_pool = []
        for b in range(BLOCKS):
            if b < BLOCKS - 1:
                block = sbuf([P, T], F32, f"val_pool{b}")
            else:
                block = last.tile([P, T], F32, name=f"val_pool{b}", align_bytes=64, offset=0)
            first_row = P * ((b + 1) % BLOCKS)
            nc.sync.dma_start(block[:], vals[first_row : first_row + P, :])
            val_pool.append(block)
            if b == 0:
                with nc.allow_non_contiguous_dma(reason="one value a partition"):
                    nc.sync.dma_start(shy_col[:], shy)
                nc.sync.dma_start(os_col[:], slot_factor.rearrange("o (p t) -> p (o t)", t=PACK))
        target_sb = sbuf([Q, E], F32, "target_sb")
        nc.sync.dma_start(target_sb[:], target)

        kg_scales = sbuf([P, I], U8, "kg_scales")
        nc.vector.tensor_copy(kg_scales[:], listed(key_scales, 0, I))

        def quantise(grouped, codes, scales):
            nc.vector.quantize_mx(
                out=codes.bitcast(FP8X4), scales=scales, in_=grouped.rearrange("p c t -> p (c t)")
            )

        q_grouped = sbuf([P, Q, PACK], BF16, "q_grouped")
        nc.scalar.copy(
            q_grouped[:].rearrange("p (c i) t -> p c t i", i=4),
            q_raw[:].rearrange("p t (c i) -> p c t i", i=4),
        )
        q_codes = sbuf([P, Q], U32, "q_codes")
        q_scales = sbuf([P, Q], U8, "q_scales")
        quantise(q_grouped[:], q_codes[:], q_scales[:])

        lam_tanh = sbuf([P, I // P, Q], F32, "lam_tanh")
        nc.vector.memset(lam_tanh[:, :, 0:1], 0.0)

        lam_rows = psum.tile([P, Q], F32, name="lam_rows", tag="bank_w")
        nc.tensor.transpose(lam_rows[:], lam_col[:].to_broadcast([Q, P]), ident[:])

        a0_banks = []
        for h in range(2):
            kg_words = sbuf([P, HALF], U32, f"kg_words{h}")
            nc.vector.tensor_copy(kg_words[:], listed(key_words, HALF * h, HALF * (h + 1)))
            a0 = psum.tile([P, 2, Q], F32, name=f"a0_{h}", tag=f"bank_a{h}")
            for j in range(2):
                slots = slice(HALF * h + P * j, HALF * h + P * (j + 1))
                nc.tensor.matmul_mx(
                    out=a0[:, j, :],
                    lhsT=kg_words[:, P * j : P * (j + 1)].bitcast(FP8X4),
                    lhsT_scale=kg_scales[:, slots],
                    rhs=q_codes[:].bitcast(FP8X4),
                    rhs_scale=q_scales[:],
                    start=True,
                    stop=True,
                )
            a0_banks.append(a0)


        a0_sb = sbuf([P, I // P, Q], F32, "a0_sb")
        tanh_sb = [sbuf([P, 2, Q], F32, f"tanh_sb{h}") for h in range(2)]
        for h in range(2):
            nc.scalar.activation(tanh_sb[h][:], a0_banks[h][:], ACT.Tanh)

        def copy_products(h):
            nc.vector.tensor_copy(a0_sb[:, 2 * h : 2 * h + 2, :], a0_banks[h][:])

        def scale_tanh(h):
            nc.vector.tensor_tensor(
                lam_tanh[:, 2 * h : 2 * h + 2, 1:Q],
                tanh_sb[h][:, :, 0 : Q - 1],
                lam_rows[:, 1:Q].unsqueeze(1).to_broadcast([P, 2, Q - 1]),
                ALU.mult,
            )

        copy_products(0)
        scale_tanh(0)
        scale_tanh(1)
        copy_products(1)
        s_banks = []
        for h, terms in enumerate(((a0_sb, lam_tanh), (lam_tanh, a0_sb))):
            s_bank = psum.tile([Q, 2, P], F32, name=f"s_{h}", tag=f"bank_s{h}")
            for n, src in enumerate(terms):
                for j in range(2):
                    nc.tensor.matmul(
                        s_bank[:, j, :],
                        src[:, 2 * h + j, :],
                        ident[:],
                        is_transpose=True,
                        start=(n == 0 and j == 0),
                        stop=(n == 1 and j == 1),
                    )
            s_banks.append(s_bank)

        neg_s = sbuf([Q, I], F32, "neg_s")
        neg_max = [sbuf([Q, 1], F32, f"neg_max{h}") for h in range(2)]
        for h in range(2):
            nc.vector.tensor_scalar(
                neg_s[:, HALF * h : HALF * (h + 1)],
                s_banks[h][:].rearrange("q j p -> q (j p)"),
                -1.0,
                None if h == 0 else neg_max[0][:],
                ALU.mult,
                ALU.min,
                accum_out=neg_max[h][:],
            )

        inv_shy = sbuf([Q, 1], F32, "inv_shy", tag="tanh_sb1")
        nc.vector.reciprocal(inv_shy[:], shy_col[:])
        neg_inv_shy = sbuf([Q, 1], F32, "neg_inv_shy")
        nc.vector.tensor_scalar(neg_inv_shy[:], inv_shy[:], -1.0, None, ALU.mult)

        def gather_on_scalar(gathered, b, first, last):
            nc.scalar.activation(gathered[:, first:last], listed(val_pool[b], first, last), ACT.Copy)

        def gather_on_vector(gathered, b, first, last):
            nc.vector.tensor_copy(gathered[:, first:last], listed(val_pool[b], first, last))

        def turn(src, bank_tag, name):
            words = src[:].bitcast(F32)
            turned = psum.tile([P, 2, P], F32, name=f"{name}_turned", tag=bank_tag)
            for u in range(2):
                nc.tensor.transpose(turned[:, u, :], words[:, u : I // 2 : 2], ident[:])
            return turned

        def weave(copy, grouped, turned):
            copy(grouped.bitcast(F32), turned[:].rearrange("p u c -> p c u"))

        gathered0 = sbuf([P, I], BF16, "gathered0", tag="tanh_sb0")
        gather_on_scalar(gathered0, 0, 0, I)
        v0_turned = turn(gathered0, "bank_a1", "v0")
        os_rows = psum.tile([P, PACK, P], F32, name="os_rows", tag="bank_s0")
        for t in range(PACK):
            nc.tensor.transpose(os_rows[:, t, :], os_col[:, t : t + 1].to_broadcast([P, P]), ident[:])
        v0_grouped = sbuf([P, P, PACK], BF16, "v0_grouped")
        weave(nc.vector.tensor_copy, v0_grouped[:], v0_turned)

        p_sb = sbuf([Q, I], F32, "p_sb", tag="val_pool0")
        p_sum = [sbuf([Q, 1], F32, f"p_sum{h}") for h in range(2)]
        run_sum = sbuf([Q, G], F32, "run_sum")
        for h in range(2):
            cols = slice(HALF * h, HALF * (h + 1))
            nc.scalar.activation(
                p_sb[:, cols], neg_s[:, cols], ACT.Exp, bias=neg_max[1][:], scale=-1.0, accum_out=p_sum[h][:]
            )
        gathered1 = sbuf([P, I], BF16, "gathered1", tag="neg_s")
        gather_on_scalar(gathered1, 1, 0, SECOND_ON_SCALAR)

        def sum_runs(h):
            nc.vector.tensor_reduce(
                run_sum[:, (G // 2) * h : (G // 2) * (h + 1)],
                p_sb[:, HALF * h : HALF * (h + 1)].rearrange("q (g r) -> q g r", r=RUN),
                AX.X,
                ALU.add,
            )

        sum_runs(0)
        total = sbuf([Q, 1], F32, "total")
        nc.vector.tensor_scalar(total[:], p_sum[0][:], p_sum[1][:], neg_inv_shy[:], ALU.add, ALU.mult)
        sum_runs(1)
        damp_rate = sbuf([Q, 1], F32, "damp_rate")
        nc.vector.reciprocal(damp_rate[:], total[:])
        gather_on_vector(gathered1, 1, SECOND_ON_SCALAR, I)
        v1_turned = turn(gathered1, "bank_a0", "v1")
        factors = sbuf([Q, I + G], F32, "factors", tag="val_pool1")
        p_os, damp = factors[:, 0:I], factors[:, I : I + G]
        nc.scalar.activation(damp, run_sum[:], ACT.Exp, scale=damp_rate[:])
        gathered2 = sbuf([P, I], BF16, "gathered2", tag="damp_rate")
        gather_on_scalar(gathered2, 2, 0, I)
        nc.vector.tensor_tensor(
            p_os.rearrange("q (p t) -> q p t", t=PACK),
            p_sb[:].rearrange("q (p t) -> q p t", t=PACK),
            os_rows[:].rearrange("q t p -> q p t"),
            ALU.mult,
        )
        damped_runs = sbuf([Q, G], F32, "damped_runs")
        damped_sum = sbuf([Q, 1], F32, "damped_sum")
        nc.vector.scalar_tensor_tensor(
            damped_runs[:], run_sum[:], 1.0, damp, ALU.mult, ALU.mult, accum_out=damped_sum[:]
        )
        v0_codes = sbuf([P, P], U32, "v0_codes", tag="damped_runs")
        v0_scales = sbuf([P, P], U8, "v0_scales")
        quantise(v0_grouped[:], v0_codes[:], v0_scales[:])
        inv_damped = sbuf([Q, 1], F32, "inv_damped")
        nc.vector.reciprocal(inv_damped[:], damped_sum[:])
        w_bf = sbuf([Q, I], BF16, "w_bf")
        nc.vector.scalar_tensor_tensor(
            w_bf[:].rearrange("q (g r) -> q g r", r=RUN),
            p_os.rearrange("q (g r) -> q g r", r=RUN),
            inv_damped[:],
            damp.unsqueeze(2).to_broadcast([Q, G, RUN]),
            ALU.mult,
            ALU.mult,
        )

        w_turned = turn(w_bf, "bank_w", "w")
        v2_turned = turn(gathered2, "bank_a1", "v2")

        gathered3 = sbuf([P, I], BF16, "gathered3", tag="inv_damped")
        gather_on_scalar(gathered3, 3, 0, LAST_ON_SCALAR)
        gather_on_vector(gathered3, 3, LAST_ON_SCALAR, I)
        v3_turned = turn(gathered3, "bank_v3", "v3")

        v1w_grouped = last.tile([P, P + Q, PACK], BF16, name="v1w_grouped", align_bytes=64, offset=4 * E)
        v2_grouped = last.tile([P, P, PACK], BF16, name="v2_grouped", align_bytes=64, offset=0)
        weave(nc.scalar.copy, v1w_grouped[:, 0:P, :], v1_turned)
        weave(nc.vector.tensor_copy, v1w_grouped[:, P : P + Q, :], w_turned)
        weave(nc.scalar.copy, v2_grouped[:], v2_turned)
        v1w_codes = sbuf([P, P + Q], U32, "v1w_codes")
        v1w_scales = sbuf([P, P + Q], U8, "v1w_scales")
        quantise(v1w_grouped[:], v1w_codes[:], v1w_scales[:])
        v2_codes = sbuf([P, P], U32, "v2_codes")
        v2_scales = sbuf([P, P], U8, "v2_scales")
        quantise(v2_grouped[:], v2_codes[:], v2_scales[:])

        def product(bank, codes, scales):
            nc.tensor.matmul_mx(
                out=bank,
                lhsT=v1w_codes[:, P : P + Q].bitcast(FP8X4),
                lhsT_scale=v1w_scales[:, P : P + Q],
                rhs=codes[:, 0:P].bitcast(FP8X4),
                rhs_scale=scales[:, 0:P],
                start=True,
                stop=True,
            )

        o_early = psum.tile([Q, E - P], F32, name="o_early", tag="bank_s1")
        for b, (codes, scales) in enumerate(
            ((v0_codes, v0_scales), (v1w_codes, v1w_scales), (v2_codes, v2_scales))
        ):
            product(o_early[:, P * b : P * (b + 1)], codes, scales)

        v3_grouped = last.tile([P, P, PACK], BF16, name="v3_grouped", align_bytes=64, offset=0)
        weave(nc.vector.tensor_copy, v3_grouped[:], v3_turned)
        v3_codes = sbuf([P, P], U32, "v3_codes")
        v3_scales = sbuf([P, P], U8, "v3_scales")
        quantise(v3_grouped[:], v3_codes[:], v3_scales[:])
        o_late = psum.tile([Q, P], F32, name="o_late", tag="bank_s0")
        product(o_late[:], v3_codes, v3_scales)

        rest = last.tile([Q, E], F32, name="rest", align_bytes=64, offset=0)
        squares = sbuf([Q, E], F32, "squares")

        def remainder(cols, bank):
            nc.vector.tensor_tensor(rest[:, cols], target_sb[:, cols], bank[:], ALU.subtract)

        def mean_square_part(cols, name):
            part = sbuf([Q, 1], F32, name)
            nc.vector.scalar_tensor_tensor(
                squares[:, cols], rest[:, cols], 1.0 / E, rest[:, cols], ALU.mult, ALU.mult, accum_out=part[:]
            )
            return part

        early_cols, late_cols = slice(P, E), slice(0, P)
        remainder(early_cols, o_early)
        mean_early = mean_square_part(early_cols, "mean_early")
        remainder(late_cols, o_late)
        base = sbuf([Q, 1], F32, "base")
        nc.vector.tensor_scalar(base[:], mean_early[:], 0.5, None, ALU.add)
        mean_late = mean_square_part(late_cols, "mean_late")
        inv_norm = sbuf([Q, 1], F32, "inv_norm")
        nc.scalar.activation(inv_norm[:], mean_late[:], ACT.Abs_reciprocal_sqrt, bias=base[:])
        result = sbuf([Q, E], F32, "result")
        nc.vector.tensor_scalar(result[:], rest[:], inv_norm[:], None, ALU.mult)
        nc.sync.dma_start(out, result[:])
